import numpy as np
CORES = [1,2,5,7,57,58,61,63,73,74,77,79]
N = 12
F = 64
def setup_inputs(rng):
    return {"a": rng.standard_normal((N, 128, 128), dtype=np.float32), "w": rng.standard_normal((N, 128, F), dtype=np.float32)}
def setup_inputs_big(rng):
    d = setup_inputs(rng)
    for k in ("a", "w"): d[k] = (d[k].astype(np.float32) * 1024.0).astype(d[k].dtype)
    return d
def setup_inputs_small(rng):
    d = setup_inputs(rng)
    for k in ("a", "w"): d[k] = (d[k].astype(np.float32) * (1 / 1024.0)).astype(d[k].dtype)
    return d
def setup_inputs_apart(rng):
    d = setup_inputs(rng)
    f = (10.0 ** rng.permutation(np.linspace(-1.5, 1.5, N))).astype(np.float32).reshape(N, 1, 1)
    for k in ("a", "w"): d[k] = (d[k].astype(np.float32) * f).astype(d[k].dtype)
    return d
def reference(a, w):
    A, W = a.astype(np.float64), w.astype(np.float64)
    p = np.stack([A[j].T @ W[j] for j in range(N)])
    return {"y": np.cumsum(p, axis=0).astype(np.float32 if a.dtype != np.float64 else np.float64)}

@@ -1,0 +1,132 @@
+from concourse.bass import DstId, RemoteDMATransfer
+from concourse.mybir import AluOpType
+
+F = 64
+PER_CHIP = 4
+N_CHIPS = 3
+ENGINES = 8
+
+SCRATCH = {
+    "asb": ("sbuf", [128, 128], "float32"),
+    "wsb": ("sbuf", [128, F], "float32"),
+    "ps": ("psum", [128, F], "float32"),
+    "p": ("sbuf", [128, F], "float32"),
+    "acc0": ("sbuf", [128, F], "float32"),
+    "acc1": ("sbuf", [128, F], "float32"),
+}
+SEMAPHORES = ["ld", "mm", "cp", "va", "st", "sent"]
+for _j in range(PER_CHIP):
+    SCRATCH["L%d" % _j] = ("sbuf", [128, F], "float32")
+    SEMAPHORES.append("q%d" % _j)
+for _h in range(N_CHIPS - 1):
+    SCRATCH["S%d" % _h] = ("sbuf", [128, F], "float32")
+    SEMAPHORES.append("t%d" % _h)
+
+
+def _groups(T, topo):
+    chips = []
+    for c in T.cores:
+        if topo.chip(c) not in chips:
+            chips.append(topo.chip(c))
+    return [[c for c in T.cores if topo.chip(c) == ch] for ch in chips]
+
+
+def _carriers(groups, gi, topo):
+    later = [d for grp in groups[gi + 1:] for d in grp]
+    able = [c for c in groups[gi] if later and all(topo.may_write(c, d) for d in later)]
+    share = {c: [] for c in able}
+    for d in later:
+        near = [c for c in able if topo.die(c) == topo.die(d)] or able
+        share[min(near, key=lambda c: len(share[c]))].append(d)
+    return share
+
+
+def _role(groups, core, topo):
+    gi = [i for i, grp in enumerate(groups) if core in grp][0]
+    grp = groups[gi]
+    q = grp.index(core)
+    share = _carriers(groups, gi, topo)
+    far = share.get(core, [])
+    first = [c for c in share if c != core]
+    rest = [c for c in grp[q + 1:] if c not in share]
+    if far:
+        first, rest = first + rest, []
+    every = first + rest + far
+    mask, n = 0, 0
+    if every:
+        m = topo.mask(core, every[0])
+        for d in every:
+            m &= topo.mask(core, d)
+        bits = [b for b in range(m.bit_length()) if (m >> b) & 1]
+        pick = bits[::max(1, len(bits) // ENGINES)][:ENGINES]
+        mask, n = sum(1 << b for b in pick), len(pick)
+    return gi, q, first, rest, far, mask, n
+
+
+def rank_program(g, core, T, topo):
+    if T.rank_of(core) is None:
+        return
+    S = T.sem
+    groups = _groups(T, topo)
+    gi, q, first, rest, far, mask, n_eng = _role(groups, core, topo)
+    grp = groups[gi]
+    v = g.vector
+
+    def engines_of(c):
+        return _role(groups, c, topo)[6]
+
+    def ids(dests):
+        return [DstId(rid=topo.addr(d)[0], pnc=topo.addr(d)[1]) for d in dests]
+
+    terms = [(T["L%d" % j], S["q%d" % j], engines_of(grp[j])) for j in range(q)]
+    for h in reversed(range(gi)):
+        bringer = [c for c, ds in _carriers(groups, h, topo).items() if core in ds][0]
+        terms.append((T["S%d" % h], S["t%d" % h], engines_of(bringer)))
+    sends = bool(first or rest or far)
+
+    g.sync.dma_start(T.asb[:], T.a[:]).then_inc(S.ld, 16)
+    g.scalar.dma_start(T.wsb[:], T.w[:]).then_inc(S.ld, 16)
+    g.tensor.wait_ge(S.ld, 32)
+    g.tensor.matmul(T.ps[:], T.asb[:], T.wsb[:], start=True, stop=True).then_inc(S.mm, 1)
+    v.wait_ge(S.mm, 1)
+    if sends or not terms:
+        v.tensor_copy(T.p[:], T.ps[:]).then_inc(S.cp, 1)
+
+    sent = 0
+    if sends:
+        g.wait_ge(S.cp, 1)
+        for dests in (first, rest):
+            if dests:
+                g.remote_dma_fused([RemoteDMATransfer(
+                    dst_ids=ids(dests), dma_engine_mask=mask, remote_sem=S["q%d" % q],
+                    srcs=[T.p[:]], dsts=[T["L%d" % q][:] for _ in dests], alu_op=0)], local_sem=S.sent)
+                sent += n_eng
+        if far:
+            for j, c in enumerate(grp):
+                if c != core:
+                    g.wait_ge(S["q%d" % j], engines_of(c))
+            g.remote_dma_fused([RemoteDMATransfer(
+                dst_ids=ids(far), dma_engine_mask=mask, remote_sem=S["t%d" % gi],
+                srcs=[T.p[:] if c == core else T["L%d" % j][:] for j, c in enumerate(grp)],
+                dsts=[T["S%d" % gi][:] for _ in far], alu_op=1)], local_sem=S.sent)
+            sent += n_eng
+        g.wait_ge(S.sent, sent)
+
+    cur = T.ps
+    for i, (buf, sem, cnt) in enumerate(terms):
+        v.wait_ge(sem, cnt)
+        if i:
+            v.wait_ge(S.va, i)
+        out = T["acc%d" % (i % 2)]
+        v.tensor_tensor(out[:], cur[:], buf[:], AluOpType.add).then_inc(S.va, 1)
+        cur = out
+
+    if terms:
+        g.sync.wait_ge(S.va, len(terms))
+    else:
+        g.sync.wait_ge(S.cp, 1)
+        cur = T.p
+    if far:
+        g.sync.wait_ge(S.sent, sent)
+    g.sync.dma_start(T.y[:], cur[:]).then_inc(S.st, 16)
+    g.sync.wait_ge(S.st, 16)

@@ -5,16 +5,20 @@ F = 64
 PER_CHIP = 4
 N_CHIPS = 3
 ENGINES = 8
+ENGINES_PASS = 16
+PRE_ADD = 1
 
 SCRATCH = {
     "asb": ("sbuf", [128, 128], "float32"),
     "wsb": ("sbuf", [128, F], "float32"),
     "ps": ("psum", [128, F], "float32"),
+    "pe": ("psum", [128, F], "float32"),
+    "pr": ("psum", [128, F], "float32"),
     "p": ("sbuf", [128, F], "float32"),
-    "acc0": ("sbuf", [128, F], "float32"),
-    "acc1": ("sbuf", [128, F], "float32"),
+    "e": ("sbuf", [128, F], "float32"),
+    "yo": ("sbuf", [128, F], "float32"),
 }
-SEMAPHORES = ["ld", "mm", "cp", "va", "st", "sent"]
+SEMAPHORES = ["ld", "mm", "cp", "va", "ev", "st", "sent"]
 for _j in range(PER_CHIP):
     SCRATCH["L%d" % _j] = ("sbuf", [128, F], "float32")
     SEMAPHORES.append("q%d" % _j)
@@ -41,48 +45,64 @@ def _carriers(groups, gi, topo):
     return share
 
 
-def _role(groups, core, topo):
-    gi = [i for i, grp in enumerate(groups) if core in grp][0]
-    grp = groups[gi]
-    q = grp.index(core)
-    share = _carriers(groups, gi, topo)
-    far = share.get(core, [])
-    first = [c for c in share if c != core]
-    rest = [c for c in grp[q + 1:] if c not in share]
-    if far:
-        first, rest = first + rest, []
-    every = first + rest + far
-    mask, n = 0, 0
-    if every:
-        m = topo.mask(core, every[0])
-        for d in every:
-            m &= topo.mask(core, d)
-        bits = [b for b in range(m.bit_length()) if (m >> b) & 1]
-        pick = bits[::max(1, len(bits) // ENGINES)][:ENGINES]
-        mask, n = sum(1 << b for b in pick), len(pick)
-    return gi, q, first, rest, far, mask, n
+def _plan(T, topo):
+    groups = _groups(T, topo)
+    near, direct, passes, bring, eng = {}, {}, {}, {}, {}
+    for gi, grp in enumerate(groups):
+        share = _carriers(groups, gi, topo)
+        for c, ds in share.items():
+            last = [d for d in ds if d in groups[-1]]
+            direct[c] = list(ds)
+            if len(ds) > 2 and len(last) > 1:
+                x, y = last[0], last[1]
+                passes[x] = (y, gi)
+                bring[(y, gi)] = x
+                direct[c] = [x] + [d for d in ds if d != x and d != y]
+            for d in direct[c]:
+                bring[(d, gi)] = c
+        for q, c in enumerate(grp):
+            turn = sorted([k for k in share if k != c], key=lambda k: (grp.index(k) - q) % len(grp))
+            near[c] = turn + [k for k in grp[q + 1:] if k not in share]
+    for c in T.cores:
+        every = near[c] + direct.get(c, []) + ([passes[c][0]] if c in passes else [])
+        eng[c] = (0, 0)
+        if every:
+            m = topo.mask(c, every[0])
+            for d in every:
+                m &= topo.mask(c, d)
+            bits = [b for b in range(m.bit_length()) if (m >> b) & 1]
+            want = ENGINES_PASS if c in passes else ENGINES
+            pick = bits[::max(1, len(bits) // want)][:want]
+            eng[c] = (sum(1 << b for b in pick), len(pick))
+    return groups, near, direct, passes, bring, eng
 
 
 def rank_program(g, core, T, topo):
     if T.rank_of(core) is None:
         return
     S = T.sem
-    groups = _groups(T, topo)
-    gi, q, first, rest, far, mask, n_eng = _role(groups, core, topo)
+    groups, near, direct, passes, bring, eng = _plan(T, topo)
+    gi = [i for i, grp in enumerate(groups) if core in grp][0]
     grp = groups[gi]
+    q = grp.index(core)
+    mask, n_eng = eng[core]
+    far = direct.get(core, [])
     v = g.vector
-
-    def engines_of(c):
-        return _role(groups, c, topo)[6]
 
     def ids(dests):
         return [DstId(rid=topo.addr(d)[0], pnc=topo.addr(d)[1]) for d in dests]
 
-    terms = [(T["L%d" % j], S["q%d" % j], engines_of(grp[j])) for j in range(q)]
-    for h in reversed(range(gi)):
-        bringer = [c for c, ds in _carriers(groups, h, topo).items() if core in ds][0]
-        terms.append((T["S%d" % h], S["t%d" % h], engines_of(bringer)))
-    sends = bool(first or rest or far)
+    def landed(j):
+        return T["L%d" % j], S["q%d" % j], eng[grp[j]][1]
+
+    def summed(h):
+        return T["S%d" % h], S["t%d" % h], eng[bring[(core, h)]][1]
+
+    got = sorted([j for j, c in enumerate(grp) if core in near[c]],
+                 key=lambda j: (near[grp[j]].index(core), topo.die(grp[j]) != topo.die(core)))
+    early, raw = (got[:PRE_ADD], got[PRE_ADD:]) if far else ([], [])
+    terms = [landed(j) for j in got if j < q] + [summed(h) for h in reversed(range(gi))]
+    sends = bool(near[core] or far or core in passes)
 
     g.sync.dma_start(T.asb[:], T.a[:]).then_inc(S.ld, 16)
     g.scalar.dma_start(T.wsb[:], T.w[:]).then_inc(S.ld, 16)
@@ -92,41 +112,65 @@ def rank_program(g, core, T, topo):
     if sends or not terms:
         v.tensor_copy(T.p[:], T.ps[:]).then_inc(S.cp, 1)
 
-    sent = 0
-    if sends:
-        g.wait_ge(S.cp, 1)
-        for dests in (first, rest):
-            if dests:
-                g.remote_dma_fused([RemoteDMATransfer(
-                    dst_ids=ids(dests), dma_engine_mask=mask, remote_sem=S["q%d" % q],
-                    srcs=[T.p[:]], dsts=[T["L%d" % q][:] for _ in dests], alu_op=0)], local_sem=S.sent)
-                sent += n_eng
-        if far:
-            for j, c in enumerate(grp):
-                if c != core:
-                    g.wait_ge(S["q%d" % j], engines_of(c))
-            g.remote_dma_fused([RemoteDMATransfer(
-                dst_ids=ids(far), dma_engine_mask=mask, remote_sem=S["t%d" % gi],
-                srcs=[T.p[:] if c == core else T["L%d" % j][:] for j, c in enumerate(grp)],
-                dsts=[T["S%d" % gi][:] for _ in far], alu_op=1)], local_sem=S.sent)
-            sent += n_eng
-        g.wait_ge(S.sent, sent)
-
+    n_va = 0
+    cur = T.ps
+    for i, j in enumerate(early):
+        buf, sem, cnt = landed(j)
+        v.wait_ge(sem, cnt)
+        if i:
+            v.wait_ge(S.va, n_va)
+        if i == len(early) - 1:
+            v.tensor_tensor(T.e[:], cur[:], buf[:], AluOpType.add).then_inc(S.ev, 1)
+        else:
+            v.tensor_tensor(T.pe[:], cur[:], buf[:], AluOpType.add).then_inc(S.va, 1)
+            n_va += 1
+            cur = T.pe
     cur = T.ps
     for i, (buf, sem, cnt) in enumerate(terms):
         v.wait_ge(sem, cnt)
         if i:
-            v.wait_ge(S.va, i)
-        out = T["acc%d" % (i % 2)]
+            v.wait_ge(S.va, n_va)
+        out = T.yo if i == len(terms) - 1 else T.pr
         v.tensor_tensor(out[:], cur[:], buf[:], AluOpType.add).then_inc(S.va, 1)
+        n_va += 1
         cur = out
 
+    sent = 0
+    if sends:
+        g.wait_ge(S.cp, 1)
+        if near[core]:
+            g.remote_dma_fused([RemoteDMATransfer(
+                dst_ids=ids(near[core]), dma_engine_mask=mask, remote_sem=S["q%d" % q],
+                srcs=[T.p[:]], dsts=[T["L%d" % q][:] for _ in near[core]], alu_op=0)], local_sem=S.sent)
+            sent += n_eng
+        if far:
+            srcs = [T.e[:] if early else T.p[:]]
+            if early:
+                g.wait_ge(S.ev, 1)
+            for j in raw:
+                buf, sem, cnt = landed(j)
+                g.wait_ge(sem, cnt)
+                srcs.append(buf[:])
+            g.remote_dma_fused([RemoteDMATransfer(
+                dst_ids=ids(far), dma_engine_mask=mask, remote_sem=S["t%d" % gi],
+                srcs=srcs, dsts=[T["S%d" % gi][:] for _ in far], alu_op=1)], local_sem=S.sent)
+            sent += n_eng
+        if core in passes:
+            nb, h = passes[core]
+            buf, sem, cnt = summed(h)
+            g.wait_ge(sem, cnt)
+            g.remote_dma_fused([RemoteDMATransfer(
+                dst_ids=ids([nb]), dma_engine_mask=mask, remote_sem=sem,
+                srcs=[buf[:]], dsts=[buf[:]], alu_op=0)], local_sem=S.sent)
+            sent += n_eng
+        g.wait_ge(S.sent, sent)
+
     if terms:
-        g.sync.wait_ge(S.va, len(terms))
+        g.sync.wait_ge(S.va, n_va)
     else:
         g.sync.wait_ge(S.cp, 1)
         cur = T.p
-    if far:
+    if far or core in passes:
         g.sync.wait_ge(S.sent, sent)
     g.sync.dma_start(T.y[:], cur[:]).then_inc(S.st, 16)
     g.sync.wait_ge(S.st, 16)

from concourse.bass import DstId, RemoteDMATransfer
from concourse.mybir import AluOpType

F = 64
PER_CHIP = 4
N_CHIPS = 3
ENGINES = 8
ENGINES_PASS = 16
PRE_ADD = 1

SCRATCH = {
    "asb": ("sbuf", [128, 128], "float32"),
    "wsb": ("sbuf", [128, F], "float32"),
    "ps": ("psum", [128, F], "float32"),
    "pe": ("psum", [128, F], "float32"),
    "pr": ("psum", [128, F], "float32"),
    "p": ("sbuf", [128, F], "float32"),
    "e": ("sbuf", [128, F], "float32"),
    "yo": ("sbuf", [128, F], "float32"),
}
SEMAPHORES = ["ld", "mm", "cp", "va", "ev", "st", "sent"]
for _j in range(PER_CHIP):
    SCRATCH["L%d" % _j] = ("sbuf", [128, F], "float32")
    SEMAPHORES.append("q%d" % _j)
for _h in range(N_CHIPS - 1):
    SCRATCH["S%d" % _h] = ("sbuf", [128, F], "float32")
    SEMAPHORES.append("t%d" % _h)


def _groups(T, topo):
    chips = []
    for c in T.cores:
        if topo.chip(c) not in chips:
            chips.append(topo.chip(c))
    return [[c for c in T.cores if topo.chip(c) == ch] for ch in chips]


def _carriers(groups, gi, topo):
    later = [d for grp in groups[gi + 1:] for d in grp]
    able = [c for c in groups[gi] if later and all(topo.may_write(c, d) for d in later)]
    share = {c: [] for c in able}
    for d in later:
        near = [c for c in able if topo.die(c) == topo.die(d)] or able
        share[min(near, key=lambda c: len(share[c]))].append(d)
    return share


def _plan(T, topo):
    groups = _groups(T, topo)
    near, direct, passes, bring, eng = {}, {}, {}, {}, {}
    for gi, grp in enumerate(groups):
        share = _carriers(groups, gi, topo)
        for c, ds in share.items():
            last = [d for d in ds if d in groups[-1]]
            direct[c] = list(ds)
            if len(ds) > 2 and len(last) > 1:
                x, y = last[0], last[1]
                passes[x] = (y, gi)
                bring[(y, gi)] = x
                direct[c] = [x] + [d for d in ds if d != x and d != y]
            for d in direct[c]:
                bring[(d, gi)] = c
        for q, c in enumerate(grp):
            turn = sorted([k for k in share if k != c], key=lambda k: (grp.index(k) - q) % len(grp))
            near[c] = turn + [k for k in grp[q + 1:] if k not in share]
    for c in T.cores:
        every = near[c] + direct.get(c, []) + ([passes[c][0]] if c in passes else [])
        eng[c] = (0, 0)
        if every:
            m = topo.mask(c, every[0])
            for d in every:
                m &= topo.mask(c, d)
            bits = [b for b in range(m.bit_length()) if (m >> b) & 1]
            want = ENGINES_PASS if c in passes else ENGINES
            pick = bits[::max(1, len(bits) // want)][:want]
            eng[c] = (sum(1 << b for b in pick), len(pick))
    return groups, near, direct, passes, bring, eng


def rank_program(g, core, T, topo):
    if T.rank_of(core) is None:
        return
    S = T.sem
    groups, near, direct, passes, bring, eng = _plan(T, topo)
    gi = [i for i, grp in enumerate(groups) if core in grp][0]
    grp = groups[gi]
    q = grp.index(core)
    mask, n_eng = eng[core]
    far = direct.get(core, [])
    v = g.vector

    def ids(dests):
        return [DstId(rid=topo.addr(d)[0], pnc=topo.addr(d)[1]) for d in dests]

    def landed(j):
        return T["L%d" % j], S["q%d" % j], eng[grp[j]][1]

    def summed(h):
        return T["S%d" % h], S["t%d" % h], eng[bring[(core, h)]][1]

    got = sorted([j for j, c in enumerate(grp) if core in near[c]],
                 key=lambda j: (near[grp[j]].index(core), topo.die(grp[j]) != topo.die(core)))
    early, raw = (got[:PRE_ADD], got[PRE_ADD:]) if far else ([], [])
    terms = [landed(j) for j in got if j < q] + [summed(h) for h in reversed(range(gi))]
    sends = bool(near[core] or far or core in passes)

    g.sync.dma_start(T.asb[:], T.a[:]).then_inc(S.ld, 16)
    g.scalar.dma_start(T.wsb[:], T.w[:]).then_inc(S.ld, 16)
    g.tensor.wait_ge(S.ld, 32)
    g.tensor.matmul(T.ps[:], T.asb[:], T.wsb[:], start=True, stop=True).then_inc(S.mm, 1)
    v.wait_ge(S.mm, 1)
    if sends or not terms:
        v.tensor_copy(T.p[:], T.ps[:]).then_inc(S.cp, 1)

    n_va = 0
    cur = T.ps
    for i, j in enumerate(early):
        buf, sem, cnt = landed(j)
        v.wait_ge(sem, cnt)
        if i:
            v.wait_ge(S.va, n_va)
        if i == len(early) - 1:
            v.tensor_tensor(T.e[:], cur[:], buf[:], AluOpType.add).then_inc(S.ev, 1)
        else:
            v.tensor_tensor(T.pe[:], cur[:], buf[:], AluOpType.add).then_inc(S.va, 1)
            n_va += 1
            cur = T.pe
    cur = T.ps
    for i, (buf, sem, cnt) in enumerate(terms):
        v.wait_ge(sem, cnt)
        if i:
            v.wait_ge(S.va, n_va)
        out = T.yo if i == len(terms) - 1 else T.pr
        v.tensor_tensor(out[:], cur[:], buf[:], AluOpType.add).then_inc(S.va, 1)
        n_va += 1
        cur = out

    sent = 0
    if sends:
        g.wait_ge(S.cp, 1)
        if near[core]:
            g.remote_dma_fused([RemoteDMATransfer(
                dst_ids=ids(near[core]), dma_engine_mask=mask, remote_sem=S["q%d" % q],
                srcs=[T.p[:]], dsts=[T["L%d" % q][:] for _ in near[core]], alu_op=0)], local_sem=S.sent)
            sent += n_eng
        if far:
            srcs = [T.e[:] if early else T.p[:]]
            if early:
                g.wait_ge(S.ev, 1)
            for j in raw:
                buf, sem, cnt = landed(j)
                g.wait_ge(sem, cnt)
                srcs.append(buf[:])
            g.remote_dma_fused([RemoteDMATransfer(
                dst_ids=ids(far), dma_engine_mask=mask, remote_sem=S["t%d" % gi],
                srcs=srcs, dsts=[T["S%d" % gi][:] for _ in far], alu_op=1)], local_sem=S.sent)
            sent += n_eng
        if core in passes:
            nb, h = passes[core]
            buf, sem, cnt = summed(h)
            g.wait_ge(sem, cnt)
            g.remote_dma_fused([RemoteDMATransfer(
                dst_ids=ids([nb]), dma_engine_mask=mask, remote_sem=sem,
                srcs=[buf[:]], dsts=[buf[:]], alu_op=0)], local_sem=S.sent)
            sent += n_eng
        g.wait_ge(S.sent, sent)

    if terms:
        g.sync.wait_ge(S.va, n_va)
    else:
        g.sync.wait_ge(S.cp, 1)
        cur = T.p
    if far or core in passes:
        g.sync.wait_ge(S.sent, sent)
    g.sync.dma_start(T.y[:], cur[:]).then_inc(S.st, 16)
    g.sync.wait_ge(S.st, 16)
